import numpy as np
import ml_dtypes


def mxq(x, axis, fmt="e4m3"):
    dtype, down = {"e4m3": (ml_dtypes.float8_e4m3fn, 7), "e5m2": (ml_dtypes.float8_e5m2, 14)}[fmt]
    v = np.moveaxis(np.asarray(x, np.float32).astype(ml_dtypes.bfloat16).astype(np.float64), axis, -1)
    blocks = v.reshape(v.shape[:-1] + (-1, 32))
    amax = np.abs(blocks).max(-1, keepdims=True)
    byte = np.maximum(np.where(amax > 0, np.frexp(amax)[1] - 1 + 127, 0) - down, 1)
    scale = np.exp2(byte - 127.0)
    codes = (blocks / scale).astype(np.float32).astype(dtype).astype(np.float64)
    return np.moveaxis((codes * scale).reshape(v.shape), -1, axis)


WIDE = False


def mx_kscale(k):
    if not WIDE:
        return np.ones(k)
    levels = np.array([10, -10, 5, -5, 0])
    if k % 512:
        return np.exp2(np.random.permutation(np.resize(levels, k // 32))).repeat(32)
    a = np.empty((k // 512, 16))
    for p in range(k // 512):
        a[p, :8] = np.random.permutation(np.resize(levels, 8))
        for g in range(8):
            far = levels[np.abs(levels - a[p, g]) >= 10]
            a[p, g + 8] = far[np.random.randint(len(far))]
    return np.exp2(a.ravel()).repeat(32)


def f64(x):
    return np.asarray(x).astype(np.float64)


def striped(idx):
    return np.tile(idx.reshape(-1, 16).T, (8, 1)).astype(np.uint16)


def unstriped(offs):
    return offs[:16].T.reshape(-1).astype(np.int64)


E2M1 = np.array([0.0, 0.5, 1.0, 1.5, 2.0, 3.0, 4.0, 6.0, -0.0, -0.5, -1.0, -1.5, -2.0, -3.0, -4.0, -6.0])


def pack_weight(w, fmt):
    k, n = w.shape
    w = f64(np.asarray(w, np.float32).astype(ml_dtypes.bfloat16)).reshape(k // 32, 32, n)
    amax = np.abs(w).max(1)
    if fmt == "e4m3":
        byte = np.frexp(amax)[1] - 1 + 127 - 7
    else:
        mant, ex = np.frexp(amax / 6.0)
        byte = np.where(mant > 0.5, ex, ex - 1) + 127
    byte = np.clip(np.where(amax > 0, byte, 1), 1, 254)
    scaled = (w * np.exp2(127.0 - byte)[:, None, :]).reshape(k, n).astype(np.float32)
    by_word = np.ascontiguousarray(scaled.reshape(k // 512, 128, 4, n).transpose(0, 1, 3, 2))
    if fmt == "e4m3":
        words = by_word.astype(ml_dtypes.float8_e4m3fn).view(np.uint8)
    else:
        c = by_word.astype(ml_dtypes.float4_e2m1fn).view(np.uint8) & 0xF
        words = (c[..., 0::2] | (c[..., 1::2] << 4)).reshape(k // 512, 128, 2 * n)
    return np.ascontiguousarray(words), np.ascontiguousarray(byte.astype(np.uint8).reshape(k // 512, 16, n))


def unpack_weight(words, scales, fmt):
    g, _, n = scales.shape
    words = np.ascontiguousarray(words).reshape(g, 128, n, -1)
    if fmt == "e4m3":
        vals = words.view(ml_dtypes.float8_e4m3fn).astype(np.float64)
    else:
        nib = np.empty((g, 128, n, 4), np.uint8)
        nib[..., 0::2] = words & 0xF
        nib[..., 1::2] = words >> 4
        vals = E2M1[nib]
    vals = vals * np.repeat(np.exp2(scales.astype(np.float64) - 127.0), 8, axis=1)[..., None]
    return vals.transpose(0, 1, 3, 2).reshape(g * 512, n)


def gelu(v):
    return 0.5 * v * (1.0 + np.tanh(np.sqrt(2.0 / np.pi) * (v + 0.044715 * v**3)))


def bf(x):
    return np.asarray(x, np.float32).astype(ml_dtypes.bfloat16)


def planes(Y):
    n, m = Y.shape
    b = f64(bf(Y)).reshape(n // 32, 32, m)
    amax = np.abs(b).max(1)
    byte = np.clip(np.where(amax > 0, np.frexp(amax)[1] - 1 + 127 - 7, 1), 1, 254)
    codes = (b * np.exp2(127.0 - byte)[:, None, :]).reshape(n, m).astype(np.float32).astype(ml_dtypes.float8_e4m3fn).view(np.uint8)
    words = codes.reshape(n // 512, 128, 4, m).transpose(0, 1, 3, 2)
    return np.ascontiguousarray(words), np.ascontiguousarray(byte.astype(np.uint8).reshape(n // 512, 16, m))


K, H, N, T, S = 1024, 512, 384, 2048, 1024


def setup_inputs():
    n = np.random.standard_normal
    s = mx_kscale(K)[:, None]
    u = mx_kscale(H)[:, None]
    tab_words, tab_scales = pack_weight(n((K, T)) * s, "e4m3")
    offs = striped(np.random.permutation(T)[:S])
    wa = (1.5 * n((K, H)) / np.sqrt(K) / s).astype(np.float32)
    wb_words, wb_scales = pack_weight(1.5 * n((K, H)) / np.sqrt(K) / s, "e2m1")
    wc_words, wc_scales = pack_weight(2.0 * n((K, H)) / np.sqrt(K) / s * u.T, "e4m3")
    wd = (n((K, N)) / np.sqrt(K) / s).astype(np.float32)
    we_words, we_scales = pack_weight(n((K, N)) / np.sqrt(K) / s, "e2m1")
    wo = (1.5 * n((H, N)) / np.sqrt(H) / u).astype(np.float32)
    return {"tab_words": tab_words, "tab_scales": tab_scales, "offs": offs, "wa": wa,
            "wb_words": wb_words, "wb_scales": wb_scales,
            "wc_words": wc_words, "wc_scales": wc_scales, "wd": wd,
            "we_words": we_words, "we_scales": we_scales, "wo": wo}


def reference(tab_words, tab_scales, offs, wa, wb_words, wb_scales, wc_words, wc_scales,
              wd, we_words, we_scales, wo):
    v = unpack_weight(tab_words, tab_scales, "e4m3")[:, unstriped(offs)]
    ga = mxq(f64(wa), 0, "e4m3").T @ v
    gb = unpack_weight(wb_words, wb_scales, "e2m1").T @ v
    val = unpack_weight(wc_words, wc_scales, "e4m3").T @ v
    h = (1 / (1 + np.exp(-ga)) - 1 / (1 + np.exp(-gb))) * val
    d = mxq(f64(wd), 0, "e4m3").T @ v
    e = unpack_weight(we_words, we_scales, "e2m1").T @ v
    y = (mxq(f64(wo), 0, "e4m3").T @ mxq(h, 0, "e4m3")) + d * e
    words, scales = planes(h)
    return y, h, words, scales

@@ -1,0 +1,314 @@
+from contextlib import ExitStack
+
+import concourse.mybir as mybir
+
+K, H, N, T, S = 1024, 512, 384, 2048, 1024
+FLOPS = 2 * S * (3 * K * H + 2 * K * N + H * N)
+
+F32 = mybir.dt.float32
+BF16 = mybir.dt.bfloat16
+I32 = mybir.dt.int32
+U32 = mybir.dt.uint32
+U16 = mybir.dt.uint16
+U8 = mybir.dt.uint8
+E4M3 = mybir.dt.float8_e4m3fn_x4
+E2M1 = mybir.dt.float4_e2m1fn_x4
+ALU = mybir.AluOpType
+SIGMOID = mybir.ActivationFunctionType.Sigmoid
+
+P = 128
+PASSES = K // 512
+HALF = 512
+QUARTER = 256
+N_TILES = N // P
+SUB_ENG = ["vector","vector","vector","vector","vector","vector","vector","vector"]
+E_ENG = ["scalar","scalar"]
+HCAST_ENG = ["scalar","scalar","scalar","vector"]
+
+
+def tile_list_pool_surveillance_kernel(
+    tc, tab_words, tab_scales, offs, wa, wb_words, wb_scales, wc_words, wc_scales,
+    wd, we_words, we_scales, wo, out_0, out_1, out_2, out_3,
+):
+    nc = tc.nc
+    with ExitStack() as ctx:
+        keep = ctx.enter_context(tc.tile_pool(name="keep", bufs=1))
+        ring = ctx.enter_context(tc.tile_pool(name="ring", bufs=2))
+        psum = ctx.enter_context(tc.psum_pool(name="psum", bufs=1))
+
+        def held(name, shape, dtype, tag=None):
+            return keep.tile(shape, dtype, name=name, tag=tag or name, align_bytes=64)
+
+        def bank(index):
+            return psum.tile([P, 512], F32, name="bank%d" % index)
+
+        offsets = keep.tile([P, S // 16], U16, name="offsets")
+        nc.sync.dma_start(offsets[:], offs)
+
+        tab_sc = held("tab_sc", [P, T], U8)
+        wb_sc_raw = held("wb_sc_raw", [P, PASSES, H], U8)
+        wc_sc_raw = held("wc_sc_raw", [P, PASSES, H], U8)
+        we_sc = held("we_sc", [P, PASSES, N], U8)
+        moved_sc = held("moved_sc", [P, S], U8)
+        nc.gpsimd.memset(tab_sc[:].bitcast(I32), 0)
+        nc.vector.memset(wb_sc_raw[:].bitcast(I32), 0)
+        nc.vector.memset(we_sc[:].bitcast(I32), 0)
+        nc.vector.memset(wc_sc_raw[:].bitcast(I32), 0)
+        nc.vector.memset(moved_sc[:].bitcast(I32), 0)
+
+        def load_scale_rows(plane, scales):
+            for q in range(4):
+                nc.sync.dma_start(
+                    out=plane[32 * q : 32 * q + 4, :, :].bitcast(I32),
+                    in_=scales[:, 4 * q : 4 * q + 4, :].rearrange("a r c -> r a c").bitcast(I32),
+                )
+
+        def load_rows(name, w, a):
+            raw = held(name, [P, 4, w.shape[1]], F32)
+            nc.sync.dma_start(out=raw[:], in_=w[512 * a : 512 * (a + 1), :].rearrange("(p j) c -> p j c", j=4))
+            return raw
+
+        wb_raw = held("wb_raw", [P, PASSES, 2 * H], U8)
+        nc.sync.dma_start(out=wb_raw[:].bitcast(I32), in_=wb_words.rearrange("a p c -> p a c").bitcast(I32))
+        for q in range(4):
+            nc.sync.dma_start(
+                out=tab_sc[32 * q : 32 * q + 8, :].bitcast(I32),
+                in_=tab_scales[:, 4 * q : 4 * q + 4, :].bitcast(I32),
+            )
+        tab_w = [held("tab_w%d" % a, [P, T], U32) for a in range(PASSES)]
+
+        def load_table_words(a):
+            nc.sync.dma_start(
+                out=tab_w[a][:].bitcast(I32), in_=tab_words[a].rearrange("p t i -> p (t i)").bitcast(I32)
+            )
+
+        load_table_words(0)
+        load_scale_rows(wb_sc_raw, wb_scales)
+        load_table_words(1)
+        got_sc = held("got_sc", [P, S], U8)
+        nc.vector.tensor_copy(out=got_sc[:], in_=tab_sc[:].indirect(offsets[:]))
+        nc.sync.dma_start(out=moved_sc[0:112, :].bitcast(I32), in_=got_sc[4:116, :].bitcast(I32))
+        wa_raw = [load_rows("wa_raw%d" % a, wa, a) for a in range(PASSES)]
+        wc_raw = held("wc_raw", [P, PASSES, H], I32)
+        nc.sync.dma_start(out=wc_raw[:], in_=wc_words.rearrange("a p c i -> p a (c i)").bitcast(I32))
+        load_scale_rows(wc_sc_raw, wc_scales)
+        we_w = held("we_w", [P, PASSES, 2 * N], U8)
+        nc.sync.dma_start(out=we_w[:].bitcast(I32), in_=we_words.rearrange("a p c -> p a c").bitcast(I32))
+        load_scale_rows(we_sc, we_scales)
+        wd_raw = [load_rows("wd_raw%d" % a, wd, a) for a in range(PASSES)]
+        wo_raw = load_rows("wo_raw", wo, 0)
+
+        got_w = [[held("got_w0%d" % a, [P, HALF], U32) for a in range(PASSES)]]
+
+        def gather(dst, window, c):
+            nc.vector.tensor_copy(out=dst[:], in_=window[:].indirect(offsets[:, 32 * c : 32 * (c + 1)]))
+
+        def table(c, a, cols):
+            plane = got_sc if a == 0 else moved_sc
+            return got_w[c][a][:, cols].bitcast(E4M3), plane[:, HALF * c + cols.start : HALF * c + cols.stop]
+
+        def deal(engine, dealt, raw):
+            engine.tensor_copy(out=dealt.rearrange("p a (t m) -> p a m t", t=4), in_=raw.rearrange("p a (m t) -> p a m t", t=4))
+
+        wb_w = held("wb_w", [P, PASSES, 2 * H], U8)
+        deal(nc.vector, wb_w[:].bitcast(U16), wb_raw[:].bitcast(U16))
+        gather(got_w[0][0], tab_w[0], 0)
+        wb_sc = held("wb_sc", [P, PASSES, H], U8)
+        deal(nc.vector, wb_sc[:], wb_sc_raw[:])
+        gather(got_w[0][1], tab_w[1], 0)
+        got_w.append([held("got_w10", [P, HALF], U32, "wb_sc_raw"), held("got_w11", [P, HALF], U32)])
+        gather(got_w[1][0], tab_w[0], 1)
+        gather(got_w[1][1], tab_w[1], 1)
+
+        sig_b = [held("sig_b%d" % c, [P, 4, HALF], F32) for c in range(2)]
+        e_sb = [held("e_sb%d" % c, [P, N_TILES, HALF], F32) for c in range(2)]
+
+        def fp4_pass(acc, words, plane, i, c, a):
+            rhs, rhs_scale = table(c, a, slice(0, HALF))
+            nc.tensor.matmul_mx(
+                out=acc[:], lhsT=words[:, a, 2 * P * i : 2 * P * (i + 1)].bitcast(E2M1),
+                lhsT_scale=plane[:, a, P * i : P * (i + 1)], rhs=rhs, rhs_scale=rhs_scale,
+                start=(a == 0), stop=(a == PASSES - 1),
+            )
+
+        def evict(acc, kind, i, c):
+            if kind == "b":
+                nc.scalar.activation(out=sig_b[c][:, i, :], in_=acc[:], func=SIGMOID)
+            elif E_ENG[c] == "scalar":
+                nc.scalar.copy(out=e_sb[c][:, i, :], in_=acc[:])
+            else:
+                nc.vector.tensor_copy(out=e_sb[c][:, i, :], in_=acc[:])
+
+        operands = {"b": (wb_w, wb_sc), "e": (we_w, we_sc)}
+
+        def fp4_group(index, kind, i, c):
+            acc = bank(index)
+            for a in range(PASSES):
+                fp4_pass(acc, operands[kind][0], operands[kind][1], i, c, a)
+            evict(acc, kind, i, c)
+
+        accs = [bank(t) for t in range(4)]
+        for a in range(PASSES):
+            for t in range(4):
+                fp4_pass(accs[t], wb_w, wb_sc, t, 0, a)
+                if a == PASSES - 1:
+                    evict(accs[t], "b", t, 0)
+        for t in range(4):
+            fp4_group(t, "b", t, 1)
+
+        def quantize(words, plane, grouped, lo, hi):
+            nc.vector.quantize_mx(
+                out=words[:, lo:hi].bitcast(E4M3), scales=plane[:, lo:hi], in_=grouped[:, 4 * lo : 4 * hi]
+            )
+
+        def cast(engine, out, in_):
+            if engine == "scalar":
+                nc.scalar.copy(out=out, in_=in_)
+            elif engine == "vector":
+                nc.vector.tensor_copy(out=out, in_=in_)
+            else:
+                nc.gpsimd.tensor_scalar(out=out, in0=in_, scalar1=1.0, scalar2=0.0, op0=ALU.mult, op1=ALU.add)
+
+        def interleave(engine, grouped, rows):
+            cast(engine, grouped.rearrange("p (c i j) -> p c j i", i=4, j=4), rows.rearrange("p j (c i) -> p c j i", i=4))
+
+        wa_g = [held("wa_g%d" % a, [P, 4 * H], BF16) for a in range(PASSES)]
+        wa_w = [held("wa_w%d" % a, [P, H], U32) for a in range(PASSES)]
+        wa_sc = [held("wa_sc%d" % a, [P, H], U8) for a in range(PASSES)]
+        for a in range(PASSES):
+            cast(["vector","vector"][a],
+                 wa_g[a][:].rearrange("p (t m j) -> p m j t", t=4, j=4),
+                 wa_raw[a][:].rearrange("p j (m t) -> p m j t", t=4))
+            quantize(wa_w[a], wa_sc[a], wa_g[a], 0, H)
+        wc_w = held("wc_w", [P, PASSES, H], I32)
+        wc_sc = held("wc_sc", [P, PASSES, H], U8)
+        deal(nc.vector, wc_w[:], wc_raw[:])
+        deal(nc.vector, wc_sc[:], wc_sc_raw[:])
+
+        def quantized_weight(engine, name, raw, tag):
+            grouped = held(name + "_g", [P, 4 * N], BF16, tag)
+            words = held(name + "_w", [P, N], U32)
+            plane = held(name + "_sc", [P, N], U8)
+            interleave(engine, grouped[:], raw[:])
+            return grouped, words, plane
+
+        def quantize_weight(w):
+            quantize(w[1], w[2], w[0], 0, 256)
+            quantize(w[1], w[2], w[0], 256, N)
+
+        h_rows = out_1.rearrange("(p t) j -> p t j", t=4)
+        y_rows = out_0.rearrange("(n p) j -> p n j", p=P)
+        h_words_out = out_2[0].rearrange("p m t -> p (m t)").bitcast(I32)
+        h_w = [held("h_w%d" % q, [P, QUARTER], U32) for q in range(4)]
+        h_sc = held("h_sc", [P, S], U8)
+        h_f = {}
+        de = {}
+
+        def cols_of(q):
+            return q // 2, slice(QUARTER * (q % 2), QUARTER * (q % 2 + 1))
+
+        def fp8_group(acc, lhs, c, cols):
+            for a in range(PASSES):
+                rhs, rhs_scale = table(c, a, cols)
+                nc.tensor.matmul_mx(out=acc, lhsT=lhs[a][0].bitcast(E4M3), lhsT_scale=lhs[a][1], rhs=rhs,
+                                    rhs_scale=rhs_scale, start=(a == 0), stop=(a == PASSES - 1))
+
+        def first_gate(c):
+            sigs = []
+            for t in range(4):
+                acc = bank(4 + t)
+                m = slice(P * t, P * (t + 1))
+                fp8_group(acc[:], [(wa_w[a][:, m], wa_sc[a][:, m]) for a in range(PASSES)], c, slice(0, HALF))
+                sig_a = ring.tile([P, HALF], F32, name="sig_a", bufs=8)
+                nc.scalar.activation(out=sig_a[:], in_=acc[:], func=SIGMOID)
+                sigs.append(sig_a)
+            return sigs
+
+        def contrast(c, sigs):
+            for t in range(4):
+                eng = nc.vector if SUB_ENG[4 * c + t] == "vector" else nc.gpsimd
+                eng.tensor_tensor(out=sig_b[c][:, t, :], in0=sigs[t][:], in1=sig_b[c][:, t, :], op=ALU.subtract)
+
+        def value(q):
+            c, cols = cols_of(q)
+            h_f[q] = held("h_f%d" % q, [P, 4, QUARTER], F32)
+            for u in range(2):
+                acc = bank(2 * (q % 2) + u)
+                for k in range(2):
+                    m = slice(P * (2 * u + k), P * (2 * u + k + 1))
+                    fp8_group(acc[:, QUARTER * k : QUARTER * (k + 1)],
+                              [(wc_w[:, a, m], wc_sc[:, a, m]) for a in range(PASSES)], c, cols)
+                nc.vector.tensor_tensor(out=h_f[q][:, 2 * u : 2 * u + 2, :], in0=sig_b[c][:, 2 * u : 2 * u + 2, cols],
+                                        in1=acc[:].rearrange("p (k j) -> p k j", k=2), op=ALU.mult)
+            nc.sync.dma_start(out=h_rows[:, :, QUARTER * q : QUARTER * (q + 1)], in_=h_f[q][:])
+
+        def quantize_h(q):
+            grouped = ring.tile([P, 4 * QUARTER], BF16, name="h_g", align_bytes=64)
+            interleave(HCAST_ENG[q], grouped[:], h_f[q][:])
+            nc.vector.quantize_mx(out=h_w[q][:].bitcast(E4M3), scales=h_sc[:, QUARTER * q : QUARTER * (q + 1)],
+                                  in_=grouped[:])
+            nc.sync.dma_start(out=h_words_out[:, QUARTER * q : QUARTER * (q + 1)], in_=h_w[q][:].bitcast(I32))
+
+        SPLIT = ((0, 2), (2, 3))
+
+        def bilinear(q, wd_q, banks):
+            c, cols = cols_of(q)
+            de[q] = ring.tile([P, N_TILES, QUARTER], F32, name="de", bufs=3)
+            for u, (lo, hi) in enumerate(SPLIT):
+                acc = bank(banks[u])
+                for n in range(lo, hi):
+                    m = slice(P * n, P * (n + 1))
+                    fp8_group(acc[:, QUARTER * (n - lo) : QUARTER * (n - lo + 1)],
+                              [(wd_q[a][1][:, m], wd_q[a][2][:, m]) for a in range(PASSES)], c, cols)
+                nc.vector.tensor_tensor(
+                    out=de[q][:, lo:hi, :], in0=e_sb[c][:, lo:hi, cols],
+                    in1=acc[:, : QUARTER * (hi - lo)].rearrange("p (k j) -> p k j", j=QUARTER), op=ALU.mult)
+
+        def scores(q, wo_q):
+            y = ring.tile([P, N_TILES, QUARTER], F32, name="y")
+            for u, (lo, hi) in enumerate(SPLIT):
+                acc = bank(2 * (q % 2) + u)
+                for n in range(lo, hi):
+                    m = slice(P * n, P * (n + 1))
+                    nc.tensor.matmul_mx(
+                        out=acc[:, QUARTER * (n - lo) : QUARTER * (n - lo + 1)], lhsT=wo_q[1][:, m].bitcast(E4M3),
+                        lhsT_scale=wo_q[2][:, m], rhs=h_w[q][:].bitcast(E4M3),
+                        rhs_scale=h_sc[:, QUARTER * q : QUARTER * (q + 1)], start=True, stop=True)
+                nc.vector.tensor_tensor(
+                    out=y[:, lo:hi, :], in0=de[q][:, lo:hi, :],
+                    in1=acc[:, : QUARTER * (hi - lo)].rearrange("p (k j) -> p k j", j=QUARTER), op=ALU.add)
+                nc.sync.dma_start(out=y_rows[:, lo:hi, QUARTER * q : QUARTER * (q + 1)], in_=y[:, lo:hi, :])
+
+
+        sigs = [first_gate(c) for c in range(2)]
+        contrast(0, sigs[0])
+        value(0)
+        value(1)
+        contrast(1, sigs[1])
+        wd_q = [quantized_weight("scalar", "wd0", wd_raw[0], "wc_raw"),
+                quantized_weight("scalar", "wd1", wd_raw[1], "wc_sc_raw")]
+        value(2)
+        value(3)
+        for n in range(N_TILES):
+            fp4_group(4 + n, "e", n, 0)
+        for w in wd_q:
+            quantize_weight(w)
+        bilinear(0, wd_q, (7, 4))
+        quantize_h(0)
+        bilinear(1, wd_q, (5, 6))
+        wo_q = quantized_weight("scalar", "wo", wo_raw, "wa_g1")
+        quantize_weight(wo_q)
+        scores(0, wo_q)
+        quantize_h(1)
+        for n in range(N_TILES):
+            fp4_group((7, 4, 5)[n], "e", n, 1)
+        scores(1, wo_q)
+        bilinear(2, wd_q, (6, 7))
+        quantize_h(2)
+        bilinear(3, wd_q, (4, 5))
+        scores(2, wo_q)
+        quantize_h(3)
+        for q in range(4):
+            nc.sync.dma_start(out=out_3[0, 4 * q : 4 * q + 4, :].bitcast(I32),
+                              in_=h_sc[32 * q : 32 * q + 4, :].bitcast(I32))
+        scores(3, wo_q)

@@ -23,7 +23,7 @@ QUARTER = 256
 N_TILES = N // P
 SUB_ENG = ["vector","vector","vector","vector","vector","vector","vector","vector"]
 E_ENG = ["scalar","scalar"]
-HCAST_ENG = ["scalar","scalar","scalar","vector"]
+HCAST_ENG = ["scalar","scalar","scalar","scalar"]
 
 
 def tile_list_pool_surveillance_kernel(
@@ -108,7 +108,7 @@ def tile_list_pool_surveillance_kernel(
             return got_w[c][a][:, cols].bitcast(E4M3), plane[:, HALF * c + cols.start : HALF * c + cols.stop]
 
         def deal(engine, dealt, raw):
-            engine.tensor_copy(out=dealt.rearrange("p a (t m) -> p a m t", t=4), in_=raw.rearrange("p a (m t) -> p a m t", t=4))
+            engine.tensor_copy(out=dealt.rearrange("p a (t m) -> p a t m", t=4), in_=raw.rearrange("p a (m t) -> p a t m", t=4))
 
         wb_w = held("wb_w", [P, PASSES, 2 * H], U8)
         deal(nc.vector, wb_w[:].bitcast(U16), wb_raw[:].bitcast(U16))
@@ -177,12 +177,13 @@ def tile_list_pool_surveillance_kernel(
         wa_sc = [held("wa_sc%d" % a, [P, H], U8) for a in range(PASSES)]
         for a in range(PASSES):
             cast(["vector","vector"][a],
-                 wa_g[a][:].rearrange("p (t m j) -> p m j t", t=4, j=4),
-                 wa_raw[a][:].rearrange("p j (m t) -> p m j t", t=4))
+                 wa_g[a][:].rearrange("p (t m j) -> p m t j", t=4, j=4),
+                 wa_raw[a][:].rearrange("p j (m t) -> p m t j", t=4))
             quantize(wa_w[a], wa_sc[a], wa_g[a], 0, H)
         wc_w = held("wc_w", [P, PASSES, H], I32)
         wc_sc = held("wc_sc", [P, PASSES, H], U8)
-        deal(nc.vector, wc_w[:], wc_raw[:])
+        nc.vector.tensor_copy(out=wc_w[:].rearrange("p a (t g i) -> p a g t i", t=4, i=4),
+                              in_=wc_raw[:].rearrange("p a (g i t) -> p a g t i", t=4, i=4))
         deal(nc.vector, wc_sc[:], wc_sc_raw[:])
 
         def quantized_weight(engine, name, raw, tag):

@@ -23,6 +23,7 @@ QUARTER = 256
 N_TILES = N // P
 SUB_ENG = ["vector","vector","vector","vector","vector","vector","vector","vector"]
 E_ENG = ["scalar","scalar"]
+DE_ON_GPSIMD = []
 HCAST_ENG = ["scalar","scalar","scalar","scalar"]
 
 
@@ -49,8 +50,10 @@ def tile_list_pool_surveillance_kernel(
         wb_sc_raw = held("wb_sc_raw", [P, PASSES, H], U8)
         wc_sc_raw = held("wc_sc_raw", [P, PASSES, H], U8)
         we_sc = held("we_sc", [P, PASSES, N], U8)
-        moved_sc = held("moved_sc", [P, S], U8)
-        nc.gpsimd.memset(tab_sc[:].bitcast(I32), 0)
+        moved_sc = held("moved_sc", [P, PASSES, S], U8)
+        nc.sync.dma_start(out=tab_sc[0:32, :].bitcast(I32), in_=tab_scales.rearrange("a q t -> q a t").bitcast(I32))
+        nc.gpsimd.memset(tab_sc[32:64, :].bitcast(I32), 0)
+        nc.gpsimd.memset(tab_sc[64:P, :].bitcast(I32), 0)
         nc.vector.memset(wb_sc_raw[:].bitcast(I32), 0)
         nc.vector.memset(we_sc[:].bitcast(I32), 0)
         nc.vector.memset(wc_sc_raw[:].bitcast(I32), 0)
@@ -70,11 +73,6 @@ def tile_list_pool_surveillance_kernel(
 
         wb_raw = held("wb_raw", [P, PASSES, 2 * H], U8)
         nc.sync.dma_start(out=wb_raw[:].bitcast(I32), in_=wb_words.rearrange("a p c -> p a c").bitcast(I32))
-        for q in range(4):
-            nc.sync.dma_start(
-                out=tab_sc[32 * q : 32 * q + 8, :].bitcast(I32),
-                in_=tab_scales[:, 4 * q : 4 * q + 4, :].bitcast(I32),
-            )
         tab_w = [held("tab_w%d" % a, [P, T], U32) for a in range(PASSES)]
 
         def load_table_words(a):
@@ -87,15 +85,18 @@ def tile_list_pool_surveillance_kernel(
         load_table_words(1)
         got_sc = held("got_sc", [P, S], U8)
         nc.vector.tensor_copy(out=got_sc[:], in_=tab_sc[:].indirect(offsets[:]))
-        nc.sync.dma_start(out=moved_sc[0:112, :].bitcast(I32), in_=got_sc[4:116, :].bitcast(I32))
+        for q in range(4):
+            nc.sync.dma_start(out=moved_sc[32 * q : 32 * q + 4, :, :].bitcast(I32),
+                              in_=got_sc[8 * q : 8 * q + 8, :].bitcast(I32))
         wa_raw = [load_rows("wa_raw%d" % a, wa, a) for a in range(PASSES)]
         wc_raw = held("wc_raw", [P, PASSES, H], I32)
         nc.sync.dma_start(out=wc_raw[:], in_=wc_words.rearrange("a p c i -> p a (c i)").bitcast(I32))
         load_scale_rows(wc_sc_raw, wc_scales)
+        wd_raw = [load_rows("wd_raw0", wd, 0)]
         we_w = held("we_w", [P, PASSES, 2 * N], U8)
         nc.sync.dma_start(out=we_w[:].bitcast(I32), in_=we_words.rearrange("a p c -> p a c").bitcast(I32))
         load_scale_rows(we_sc, we_scales)
-        wd_raw = [load_rows("wd_raw%d" % a, wd, a) for a in range(PASSES)]
+        wd_raw.append(load_rows("wd_raw1", wd, 1))
         wo_raw = load_rows("wo_raw", wo, 0)
 
         got_w = [[held("got_w0%d" % a, [P, HALF], U32) for a in range(PASSES)]]
@@ -104,8 +105,7 @@ def tile_list_pool_surveillance_kernel(
             nc.vector.tensor_copy(out=dst[:], in_=window[:].indirect(offsets[:, 32 * c : 32 * (c + 1)]))
 
         def table(c, a, cols):
-            plane = got_sc if a == 0 else moved_sc
-            return got_w[c][a][:, cols].bitcast(E4M3), plane[:, HALF * c + cols.start : HALF * c + cols.stop]
+            return got_w[c][a][:, cols].bitcast(E4M3), moved_sc[:, a, HALF * c + cols.start : HALF * c + cols.stop]
 
         def deal(engine, dealt, raw):
             engine.tensor_copy(out=dealt.rearrange("p a (t m) -> p a t m", t=4), in_=raw.rearrange("p a (m t) -> p a t m", t=4))
@@ -170,6 +170,9 @@ def tile_list_pool_surveillance_kernel(
                 nc.gpsimd.tensor_scalar(out=out, in0=in_, scalar1=1.0, scalar2=0.0, op0=ALU.mult, op1=ALU.add)
 
         def interleave(engine, grouped, rows):
+            if engine == "gpsimd":
+                cast(engine, grouped.rearrange("p (c j) -> p c j", j=4), rows.rearrange("p j c -> p c j"))
+                return
             cast(engine, grouped.rearrange("p (c i j) -> p c j i", i=4, j=4), rows.rearrange("p j (c i) -> p c j i", i=4))
 
         wa_g = [held("wa_g%d" % a, [P, 4 * H], BF16) for a in range(PASSES)]
@@ -190,7 +193,10 @@ def tile_list_pool_surveillance_kernel(
             grouped = held(name + "_g", [P, 4 * N], BF16, tag)
             words = held(name + "_w", [P, N], U32)
             plane = held(name + "_sc", [P, N], U8)
-            interleave(engine, grouped[:], raw[:])
+            pieces = 3 if engine == "gpsimd" else 1
+            for i in range(pieces):
+                w = N // pieces
+                interleave(engine, grouped[:, 4 * w * i : 4 * w * (i + 1)], raw[:, :, w * i : w * (i + 1)])
             return grouped, words, plane
 
         def quantize_weight(w):
@@ -220,7 +226,7 @@ def tile_list_pool_surveillance_kernel(
                 acc = bank(4 + t)
                 m = slice(P * t, P * (t + 1))
                 fp8_group(acc[:], [(wa_w[a][:, m], wa_sc[a][:, m]) for a in range(PASSES)], c, slice(0, HALF))
-                sig_a = ring.tile([P, HALF], F32, name="sig_a", bufs=8)
+                sig_a = held("sig_a%d%d" % (c, t), [P, HALF], F32)
                 nc.scalar.activation(out=sig_a[:], in_=acc[:], func=SIGMOID)
                 sigs.append(sig_a)
             return sigs
@@ -252,18 +258,13 @@ def tile_list_pool_surveillance_kernel(
 
         SPLIT = ((0, 2), (2, 3))
 
-        def bilinear(q, wd_q, banks):
-            c, cols = cols_of(q)
-            de[q] = ring.tile([P, N_TILES, QUARTER], F32, name="de", bufs=3)
-            for u, (lo, hi) in enumerate(SPLIT):
-                acc = bank(banks[u])
-                for n in range(lo, hi):
-                    m = slice(P * n, P * (n + 1))
-                    fp8_group(acc[:, QUARTER * (n - lo) : QUARTER * (n - lo + 1)],
-                              [(wd_q[a][1][:, m], wd_q[a][2][:, m]) for a in range(PASSES)], c, cols)
-                nc.vector.tensor_tensor(
-                    out=de[q][:, lo:hi, :], in0=e_sb[c][:, lo:hi, cols],
-                    in1=acc[:, : QUARTER * (hi - lo)].rearrange("p (k j) -> p k j", j=QUARTER), op=ALU.mult)
+        def bilinear(c, banks):
+            de[c] = held("de%d" % c, [P, N_TILES, HALF], F32)
+            for n in range(N_TILES):
+                acc = bank(banks[n])
+                ms = [slice(N * a + P * n, N * a + P * (n + 1)) for a in range(PASSES)]
+                fp8_group(acc[:], [(wd_w[:, m], wd_sc[:, m]) for m in ms], c, slice(0, HALF))
+                nc.vector.tensor_tensor(out=de[c][:, n, :], in0=e_sb[c][:, n, :], in1=acc[:], op=ALU.mult)
 
         def scores(q, wo_q):
             y = ring.tile([P, N_TILES, QUARTER], F32, name="y")
@@ -276,7 +277,7 @@ def tile_list_pool_surveillance_kernel(
                         lhsT_scale=wo_q[2][:, m], rhs=h_w[q][:].bitcast(E4M3),
                         rhs_scale=h_sc[:, QUARTER * q : QUARTER * (q + 1)], start=True, stop=True)
                 nc.vector.tensor_tensor(
-                    out=y[:, lo:hi, :], in0=de[q][:, lo:hi, :],
+                    out=y[:, lo:hi, :], in0=de[q // 2][:, lo:hi, cols_of(q)[1]],
                     in1=acc[:, : QUARTER * (hi - lo)].rearrange("p (k j) -> p k j", j=QUARTER), op=ALU.add)
                 nc.sync.dma_start(out=y_rows[:, lo:hi, QUARTER * q : QUARTER * (q + 1)], in_=y[:, lo:hi, :])
 
@@ -286,30 +287,31 @@ def tile_list_pool_surveillance_kernel(
         value(0)
         value(1)
         contrast(1, sigs[1])
-        wd_q = [quantized_weight("scalar", "wd0", wd_raw[0], "wc_raw"),
-                quantized_weight("scalar", "wd1", wd_raw[1], "wc_sc_raw")]
+        wd_g = held("wd_g", [P, PASSES * 4 * N], BF16, "wc_raw")
+        wd_w = held("wd_w", [P, PASSES * N], U32)
+        wd_sc = held("wd_sc", [P, PASSES * N], U8)
+        for a in range(PASSES):
+            interleave("scalar", wd_g[:, 4 * N * a : 4 * N * (a + 1)], wd_raw[a][:])
         value(2)
         value(3)
         for n in range(N_TILES):
             fp4_group(4 + n, "e", n, 0)
-        for w in wd_q:
-            quantize_weight(w)
-        bilinear(0, wd_q, (7, 4))
+        quantize(wd_w, wd_sc, wd_g, 0, 512)
+        quantize(wd_w, wd_sc, wd_g, 512, PASSES * N)
+        bilinear(0, (7, 4, 5))
         quantize_h(0)
-        bilinear(1, wd_q, (5, 6))
         wo_q = quantized_weight("scalar", "wo", wo_raw, "wa_g1")
         quantize_weight(wo_q)
-        scores(0, wo_q)
         quantize_h(1)
         for n in range(N_TILES):
-            fp4_group((7, 4, 5)[n], "e", n, 1)
+            fp4_group((6, 7, 4)[n], "e", n, 1)
+        scores(0, wo_q)
         scores(1, wo_q)
-        bilinear(2, wd_q, (6, 7))
+        bilinear(1, (5, 6, 7))
         quantize_h(2)
-        bilinear(3, wd_q, (4, 5))
-        scores(2, wo_q)
         quantize_h(3)
         for q in range(4):
             nc.sync.dma_start(out=out_3[0, 4 * q : 4 * q + 4, :].bitcast(I32),
                               in_=h_sc[32 * q : 32 * q + 4, :].bitcast(I32))
+        scores(2, wo_q)
         scores(3, wo_q)

from contextlib import ExitStack

import concourse.mybir as mybir

K, H, N, T, S = 1024, 512, 384, 2048, 1024
FLOPS = 2 * S * (3 * K * H + 2 * K * N + H * N)

F32 = mybir.dt.float32
BF16 = mybir.dt.bfloat16
I32 = mybir.dt.int32
U32 = mybir.dt.uint32
U16 = mybir.dt.uint16
U8 = mybir.dt.uint8
E4M3 = mybir.dt.float8_e4m3fn_x4
E2M1 = mybir.dt.float4_e2m1fn_x4
ALU = mybir.AluOpType
SIGMOID = mybir.ActivationFunctionType.Sigmoid

P = 128
PASSES = K // 512
HALF = 512
QUARTER = 256
N_TILES = N // P
SUB_ENG = ["vector","vector","vector","vector","vector","vector","vector","vector"]
E_ENG = ["scalar","scalar"]
DE_ON_GPSIMD = []
HCAST_ENG = ["scalar","scalar","scalar","scalar"]


def tile_list_pool_surveillance_kernel(
    tc, tab_words, tab_scales, offs, wa, wb_words, wb_scales, wc_words, wc_scales,
    wd, we_words, we_scales, wo, out_0, out_1, out_2, out_3,
):
    nc = tc.nc
    with ExitStack() as ctx:
        keep = ctx.enter_context(tc.tile_pool(name="keep", bufs=1))
        ring = ctx.enter_context(tc.tile_pool(name="ring", bufs=2))
        psum = ctx.enter_context(tc.psum_pool(name="psum", bufs=1))

        def held(name, shape, dtype, tag=None):
            return keep.tile(shape, dtype, name=name, tag=tag or name, align_bytes=64)

        def bank(index):
            return psum.tile([P, 512], F32, name="bank%d" % index)

        offsets = keep.tile([P, S // 16], U16, name="offsets")
        nc.sync.dma_start(offsets[:], offs)

        tab_sc = held("tab_sc", [P, T], U8)
        wb_sc_raw = held("wb_sc_raw", [P, PASSES, H], U8)
        wc_sc_raw = held("wc_sc_raw", [P, PASSES, H], U8)
        we_sc = held("we_sc", [P, PASSES, N], U8)
        moved_sc = held("moved_sc", [P, PASSES, S], U8)
        nc.sync.dma_start(out=tab_sc[0:32, :].bitcast(I32), in_=tab_scales.rearrange("a q t -> q a t").bitcast(I32))
        nc.gpsimd.memset(tab_sc[32:64, :].bitcast(I32), 0)
        nc.gpsimd.memset(tab_sc[64:P, :].bitcast(I32), 0)
        nc.vector.memset(wb_sc_raw[:].bitcast(I32), 0)
        nc.vector.memset(we_sc[:].bitcast(I32), 0)
        nc.vector.memset(wc_sc_raw[:].bitcast(I32), 0)
        nc.vector.memset(moved_sc[:].bitcast(I32), 0)

        def load_scale_rows(plane, scales):
            for q in range(4):
                nc.sync.dma_start(
                    out=plane[32 * q : 32 * q + 4, :, :].bitcast(I32),
                    in_=scales[:, 4 * q : 4 * q + 4, :].rearrange("a r c -> r a c").bitcast(I32),
                )

        def load_rows(name, w, a):
            raw = held(name, [P, 4, w.shape[1]], F32)
            nc.sync.dma_start(out=raw[:], in_=w[512 * a : 512 * (a + 1), :].rearrange("(p j) c -> p j c", j=4))
            return raw

        wb_raw = held("wb_raw", [P, PASSES, 2 * H], U8)
        nc.sync.dma_start(out=wb_raw[:].bitcast(I32), in_=wb_words.rearrange("a p c -> p a c").bitcast(I32))
        tab_w = [held("tab_w%d" % a, [P, T], U32) for a in range(PASSES)]

        def load_table_words(a):
            nc.sync.dma_start(
                out=tab_w[a][:].bitcast(I32), in_=tab_words[a].rearrange("p t i -> p (t i)").bitcast(I32)
            )

        load_table_words(0)
        load_scale_rows(wb_sc_raw, wb_scales)
        load_table_words(1)
        got_sc = held("got_sc", [P, S], U8)
        nc.vector.tensor_copy(out=got_sc[:], in_=tab_sc[:].indirect(offsets[:]))
        for q in range(4):
            nc.sync.dma_start(out=moved_sc[32 * q : 32 * q + 4, :, :].bitcast(I32),
                              in_=got_sc[8 * q : 8 * q + 8, :].bitcast(I32))
        wa_raw = [load_rows("wa_raw%d" % a, wa, a) for a in range(PASSES)]
        wc_raw = held("wc_raw", [P, PASSES, H], I32)
        nc.sync.dma_start(out=wc_raw[:], in_=wc_words.rearrange("a p c i -> p a (c i)").bitcast(I32))
        load_scale_rows(wc_sc_raw, wc_scales)
        wd_raw = [load_rows("wd_raw0", wd, 0)]
        we_w = held("we_w", [P, PASSES, 2 * N], U8)
        nc.sync.dma_start(out=we_w[:].bitcast(I32), in_=we_words.rearrange("a p c -> p a c").bitcast(I32))
        load_scale_rows(we_sc, we_scales)
        wd_raw.append(load_rows("wd_raw1", wd, 1))
        wo_raw = load_rows("wo_raw", wo, 0)

        got_w = [[held("got_w0%d" % a, [P, HALF], U32) for a in range(PASSES)]]

        def gather(dst, window, c):
            nc.vector.tensor_copy(out=dst[:], in_=window[:].indirect(offsets[:, 32 * c : 32 * (c + 1)]))

        def table(c, a, cols):
            return got_w[c][a][:, cols].bitcast(E4M3), moved_sc[:, a, HALF * c + cols.start : HALF * c + cols.stop]

        def deal(engine, dealt, raw):
            engine.tensor_copy(out=dealt.rearrange("p a (t m) -> p a t m", t=4), in_=raw.rearrange("p a (m t) -> p a t m", t=4))

        wb_w = held("wb_w", [P, PASSES, 2 * H], U8)
        deal(nc.vector, wb_w[:].bitcast(U16), wb_raw[:].bitcast(U16))
        gather(got_w[0][0], tab_w[0], 0)
        wb_sc = held("wb_sc", [P, PASSES, H], U8)
        deal(nc.vector, wb_sc[:], wb_sc_raw[:])
        gather(got_w[0][1], tab_w[1], 0)
        got_w.append([held("got_w10", [P, HALF], U32, "wb_sc_raw"), held("got_w11", [P, HALF], U32)])
        gather(got_w[1][0], tab_w[0], 1)
        gather(got_w[1][1], tab_w[1], 1)

        sig_b = [held("sig_b%d" % c, [P, 4, HALF], F32) for c in range(2)]
        e_sb = [held("e_sb%d" % c, [P, N_TILES, HALF], F32) for c in range(2)]

        def fp4_pass(acc, words, plane, i, c, a):
            rhs, rhs_scale = table(c, a, slice(0, HALF))
            nc.tensor.matmul_mx(
                out=acc[:], lhsT=words[:, a, 2 * P * i : 2 * P * (i + 1)].bitcast(E2M1),
                lhsT_scale=plane[:, a, P * i : P * (i + 1)], rhs=rhs, rhs_scale=rhs_scale,
                start=(a == 0), stop=(a == PASSES - 1),
            )

        def evict(acc, kind, i, c):
            if kind == "b":
                nc.scalar.activation(out=sig_b[c][:, i, :], in_=acc[:], func=SIGMOID)
            elif E_ENG[c] == "scalar":
                nc.scalar.copy(out=e_sb[c][:, i, :], in_=acc[:])
            else:
                nc.vector.tensor_copy(out=e_sb[c][:, i, :], in_=acc[:])

        operands = {"b": (wb_w, wb_sc), "e": (we_w, we_sc)}

        def fp4_group(index, kind, i, c):
            acc = bank(index)
            for a in range(PASSES):
                fp4_pass(acc, operands[kind][0], operands[kind][1], i, c, a)
            evict(acc, kind, i, c)

        accs = [bank(t) for t in range(4)]
        for a in range(PASSES):
            for t in range(4):
                fp4_pass(accs[t], wb_w, wb_sc, t, 0, a)
                if a == PASSES - 1:
                    evict(accs[t], "b", t, 0)
        for t in range(4):
            fp4_group(t, "b", t, 1)

        def quantize(words, plane, grouped, lo, hi):
            nc.vector.quantize_mx(
                out=words[:, lo:hi].bitcast(E4M3), scales=plane[:, lo:hi], in_=grouped[:, 4 * lo : 4 * hi]
            )

        def cast(engine, out, in_):
            if engine == "scalar":
                nc.scalar.copy(out=out, in_=in_)
            elif engine == "vector":
                nc.vector.tensor_copy(out=out, in_=in_)
            else:
                nc.gpsimd.tensor_scalar(out=out, in0=in_, scalar1=1.0, scalar2=0.0, op0=ALU.mult, op1=ALU.add)

        def interleave(engine, grouped, rows):
            if engine == "gpsimd":
                cast(engine, grouped.rearrange("p (c j) -> p c j", j=4), rows.rearrange("p j c -> p c j"))
                return
            cast(engine, grouped.rearrange("p (c i j) -> p c j i", i=4, j=4), rows.rearrange("p j (c i) -> p c j i", i=4))

        wa_g = [held("wa_g%d" % a, [P, 4 * H], BF16) for a in range(PASSES)]
        wa_w = [held("wa_w%d" % a, [P, H], U32) for a in range(PASSES)]
        wa_sc = [held("wa_sc%d" % a, [P, H], U8) for a in range(PASSES)]
        for a in range(PASSES):
            cast(["vector","vector"][a],
                 wa_g[a][:].rearrange("p (t m j) -> p m t j", t=4, j=4),
                 wa_raw[a][:].rearrange("p j (m t) -> p m t j", t=4))
            quantize(wa_w[a], wa_sc[a], wa_g[a], 0, H)
        wc_w = held("wc_w", [P, PASSES, H], I32)
        wc_sc = held("wc_sc", [P, PASSES, H], U8)
        nc.vector.tensor_copy(out=wc_w[:].rearrange("p a (t g i) -> p a g t i", t=4, i=4),
                              in_=wc_raw[:].rearrange("p a (g i t) -> p a g t i", t=4, i=4))
        deal(nc.vector, wc_sc[:], wc_sc_raw[:])

        def quantized_weight(engine, name, raw, tag):
            grouped = held(name + "_g", [P, 4 * N], BF16, tag)
            words = held(name + "_w", [P, N], U32)
            plane = held(name + "_sc", [P, N], U8)
            pieces = 3 if engine == "gpsimd" else 1
            for i in range(pieces):
                w = N // pieces
                interleave(engine, grouped[:, 4 * w * i : 4 * w * (i + 1)], raw[:, :, w * i : w * (i + 1)])
            return grouped, words, plane

        def quantize_weight(w):
            quantize(w[1], w[2], w[0], 0, 256)
            quantize(w[1], w[2], w[0], 256, N)

        h_rows = out_1.rearrange("(p t) j -> p t j", t=4)
        y_rows = out_0.rearrange("(n p) j -> p n j", p=P)
        h_words_out = out_2[0].rearrange("p m t -> p (m t)").bitcast(I32)
        h_w = [held("h_w%d" % q, [P, QUARTER], U32) for q in range(4)]
        h_sc = held("h_sc", [P, S], U8)
        h_f = {}
        de = {}

        def cols_of(q):
            return q // 2, slice(QUARTER * (q % 2), QUARTER * (q % 2 + 1))

        def fp8_group(acc, lhs, c, cols):
            for a in range(PASSES):
                rhs, rhs_scale = table(c, a, cols)
                nc.tensor.matmul_mx(out=acc, lhsT=lhs[a][0].bitcast(E4M3), lhsT_scale=lhs[a][1], rhs=rhs,
                                    rhs_scale=rhs_scale, start=(a == 0), stop=(a == PASSES - 1))

        def first_gate(c):
            sigs = []
            for t in range(4):
                acc = bank(4 + t)
                m = slice(P * t, P * (t + 1))
                fp8_group(acc[:], [(wa_w[a][:, m], wa_sc[a][:, m]) for a in range(PASSES)], c, slice(0, HALF))
                sig_a = held("sig_a%d%d" % (c, t), [P, HALF], F32)
                nc.scalar.activation(out=sig_a[:], in_=acc[:], func=SIGMOID)
                sigs.append(sig_a)
            return sigs

        def contrast(c, sigs):
            for t in range(4):
                eng = nc.vector if SUB_ENG[4 * c + t] == "vector" else nc.gpsimd
                eng.tensor_tensor(out=sig_b[c][:, t, :], in0=sigs[t][:], in1=sig_b[c][:, t, :], op=ALU.subtract)

        def value(q):
            c, cols = cols_of(q)
            h_f[q] = held("h_f%d" % q, [P, 4, QUARTER], F32)
            for u in range(2):
                acc = bank(2 * (q % 2) + u)
                for k in range(2):
                    m = slice(P * (2 * u + k), P * (2 * u + k + 1))
                    fp8_group(acc[:, QUARTER * k : QUARTER * (k + 1)],
                              [(wc_w[:, a, m], wc_sc[:, a, m]) for a in range(PASSES)], c, cols)
                nc.vector.tensor_tensor(out=h_f[q][:, 2 * u : 2 * u + 2, :], in0=sig_b[c][:, 2 * u : 2 * u + 2, cols],
                                        in1=acc[:].rearrange("p (k j) -> p k j", k=2), op=ALU.mult)
            nc.sync.dma_start(out=h_rows[:, :, QUARTER * q : QUARTER * (q + 1)], in_=h_f[q][:])

        def quantize_h(q):
            grouped = ring.tile([P, 4 * QUARTER], BF16, name="h_g", align_bytes=64)
            interleave(HCAST_ENG[q], grouped[:], h_f[q][:])
            nc.vector.quantize_mx(out=h_w[q][:].bitcast(E4M3), scales=h_sc[:, QUARTER * q : QUARTER * (q + 1)],
                                  in_=grouped[:])
            nc.sync.dma_start(out=h_words_out[:, QUARTER * q : QUARTER * (q + 1)], in_=h_w[q][:].bitcast(I32))

        SPLIT = ((0, 2), (2, 3))

        def bilinear(c, banks):
            de[c] = held("de%d" % c, [P, N_TILES, HALF], F32)
            for n in range(N_TILES):
                acc = bank(banks[n])
                ms = [slice(N * a + P * n, N * a + P * (n + 1)) for a in range(PASSES)]
                fp8_group(acc[:], [(wd_w[:, m], wd_sc[:, m]) for m in ms], c, slice(0, HALF))
                nc.vector.tensor_tensor(out=de[c][:, n, :], in0=e_sb[c][:, n, :], in1=acc[:], op=ALU.mult)

        def scores(q, wo_q):
            y = ring.tile([P, N_TILES, QUARTER], F32, name="y")
            for u, (lo, hi) in enumerate(SPLIT):
                acc = bank(2 * (q % 2) + u)
                for n in range(lo, hi):
                    m = slice(P * n, P * (n + 1))
                    nc.tensor.matmul_mx(
                        out=acc[:, QUARTER * (n - lo) : QUARTER * (n - lo + 1)], lhsT=wo_q[1][:, m].bitcast(E4M3),
                        lhsT_scale=wo_q[2][:, m], rhs=h_w[q][:].bitcast(E4M3),
                        rhs_scale=h_sc[:, QUARTER * q : QUARTER * (q + 1)], start=True, stop=True)
                nc.vector.tensor_tensor(
                    out=y[:, lo:hi, :], in0=de[q // 2][:, lo:hi, cols_of(q)[1]],
                    in1=acc[:, : QUARTER * (hi - lo)].rearrange("p (k j) -> p k j", j=QUARTER), op=ALU.add)
                nc.sync.dma_start(out=y_rows[:, lo:hi, QUARTER * q : QUARTER * (q + 1)], in_=y[:, lo:hi, :])


        sigs = [first_gate(c) for c in range(2)]
        contrast(0, sigs[0])
        value(0)
        value(1)
        contrast(1, sigs[1])
        wd_g = held("wd_g", [P, PASSES * 4 * N], BF16, "wc_raw")
        wd_w = held("wd_w", [P, PASSES * N], U32)
        wd_sc = held("wd_sc", [P, PASSES * N], U8)
        for a in range(PASSES):
            interleave("scalar", wd_g[:, 4 * N * a : 4 * N * (a + 1)], wd_raw[a][:])
        value(2)
        value(3)
        for n in range(N_TILES):
            fp4_group(4 + n, "e", n, 0)
        quantize(wd_w, wd_sc, wd_g, 0, 512)
        quantize(wd_w, wd_sc, wd_g, 512, PASSES * N)
        bilinear(0, (7, 4, 5))
        quantize_h(0)
        wo_q = quantized_weight("scalar", "wo", wo_raw, "wa_g1")
        quantize_weight(wo_q)
        quantize_h(1)
        for n in range(N_TILES):
            fp4_group((6, 7, 4)[n], "e", n, 1)
        scores(0, wo_q)
        scores(1, wo_q)
        bilinear(1, (5, 6, 7))
        quantize_h(2)
        quantize_h(3)
        for q in range(4):
            nc.sync.dma_start(out=out_3[0, 4 * q : 4 * q + 4, :].bitcast(I32),
                              in_=h_sc[32 * q : 32 * q + 4, :].bitcast(I32))
        scores(2, wo_q)
        scores(3, wo_q)
